import numpy as np
import ml_dtypes


def mxq(x, axis, fmt="e4m3"):
    dtype, down = {"e4m3": (ml_dtypes.float8_e4m3fn, 7), "e5m2": (ml_dtypes.float8_e5m2, 14)}[fmt]
    v = np.moveaxis(np.asarray(x, np.float32).astype(ml_dtypes.bfloat16).astype(np.float64), axis, -1)
    blocks = v.reshape(v.shape[:-1] + (-1, 32))
    amax = np.abs(blocks).max(-1, keepdims=True)
    byte = np.maximum(np.where(amax > 0, np.frexp(amax)[1] - 1 + 127, 0) - down, 1)
    scale = np.exp2(byte - 127.0)
    codes = (blocks / scale).astype(np.float32).astype(dtype).astype(np.float64)
    return np.moveaxis((codes * scale).reshape(v.shape), -1, axis)


WIDE = False


def mx_kscale(k):
    if not WIDE:
        return np.ones(k)
    levels = np.array([10, -10, 5, -5, 0])
    if k % 512:
        return np.exp2(np.random.permutation(np.resize(levels, k // 32))).repeat(32)
    a = np.empty((k // 512, 16))
    for p in range(k // 512):
        a[p, :8] = np.random.permutation(np.resize(levels, 8))
        for g in range(8):
            far = levels[np.abs(levels - a[p, g]) >= 10]
            a[p, g + 8] = far[np.random.randint(len(far))]
    return np.exp2(a.ravel()).repeat(32)


def f64(x):
    return np.asarray(x).astype(np.float64)


def striped(idx):
    return np.tile(idx.reshape(-1, 16).T, (8, 1)).astype(np.uint16)


def unstriped(offs):
    return offs[:16].T.reshape(-1).astype(np.int64)


E2M1 = np.array([0.0, 0.5, 1.0, 1.5, 2.0, 3.0, 4.0, 6.0, -0.0, -0.5, -1.0, -1.5, -2.0, -3.0, -4.0, -6.0])


def pack_fp4(w):
    k, n = w.shape
    w = f64(np.asarray(w, np.float32).astype(ml_dtypes.bfloat16)).reshape(k // 32, 32, n)
    amax = np.abs(w).max(1)
    mant, ex = np.frexp(amax / 6.0)
    byte = np.clip(np.where(amax > 0, np.where(mant > 0.5, ex, ex - 1) + 127, 1), 1, 254)
    scaled = (w * np.exp2(127.0 - byte)[:, None, :]).reshape(k, n).astype(np.float32)
    c = np.ascontiguousarray(scaled.reshape(k // 512, 128, 4, n).transpose(0, 1, 3, 2)).astype(ml_dtypes.float4_e2m1fn).view(np.uint8) & 0xF
    words = (c[..., 0::2] | (c[..., 1::2] << 4)).reshape(k // 512, 128, 2 * n)
    return np.ascontiguousarray(words), np.ascontiguousarray(byte.astype(np.uint8).reshape(k // 512, 16, n))


def unpack_fp4(words, scales):
    g, _, n = scales.shape
    words = np.ascontiguousarray(words).reshape(g, 128, n, 2)
    nib = np.empty((g, 128, n, 4), np.uint8)
    nib[..., 0::2] = words & 0xF
    nib[..., 1::2] = words >> 4
    vals = E2M1[nib] * np.repeat(np.exp2(scales.astype(np.float64) - 127.0), 8, axis=1)[..., None]
    return vals.transpose(0, 1, 3, 2).reshape(g * 512, n)


K, T, S, V, N = 512, 4096, 1536, 512, 256


def setup_inputs():
    n = np.random.standard_normal
    s = mx_kscale(K)[:, None]
    packed_w1 = pack_fp4(n((K, N)) / np.sqrt(K) / s)
    packed_w2 = pack_fp4(n((K, N)) / np.sqrt(K) / s)
    return {
        "xT": (n((K, T)) * s).astype(np.float32),
        "w1_words": packed_w1[0],
        "w1_scales": packed_w1[1],
        "w2_words": packed_w2[0],
        "w2_scales": packed_w2[1],
        "offs": striped(np.random.permutation(T)[:S]),
    }


def reference(xT, w1_words, w1_scales, w2_words, w2_scales, offs):
    xq = mxq(f64(xT)[:, unstriped(offs)], 0, "e4m3")
    e = np.exp(unpack_fp4(w1_words, w1_scales).T @ xq)
    h = unpack_fp4(w2_words, w2_scales).T @ xq
    num = e[:, :V] * h[:, :V] + e[:, V:2 * V] * h[:, V:2 * V] + e[:, 2 * V:3 * V] * h[:, 2 * V:3 * V]
    den = e[:, :V] + e[:, V:2 * V] + e[:, 2 * V:3 * V]
    return num / den

@@ -1,0 +1,138 @@
+from contextlib import ExitStack
+
+import concourse.mybir as mybir
+
+K, T, S, V, N = 512, 4096, 1536, 512, 256
+FLOPS = 2 * K * S * 2 * N
+
+F32 = mybir.dt.float32
+BF16 = mybir.dt.bfloat16
+I32 = mybir.dt.int32
+U32 = mybir.dt.uint32
+U16 = mybir.dt.uint16
+U8 = mybir.dt.uint8
+FP8X4 = mybir.dt.float8_e4m3fn_x4
+FP4X4 = mybir.dt.float4_e2m1fn_x4
+ALU = mybir.AluOpType
+ACT = mybir.ActivationFunctionType
+
+P = 128
+PACK = 4
+D = 3
+
+CHUNKS = ([2048, 2048], [2048, 2048], [2048, 2048], [2048, 1024, 512, 512])
+
+
+def tile_picked_apool_none_e_kernel(tc, xT, w1_words, w1_scales, w2_words, w2_scales, offs, out):
+    nc = tc.nc
+    with ExitStack() as ctx:
+        keep = ctx.enter_context(tc.tile_pool(name="keep", bufs=1))
+        psum = ctx.enter_context(tc.psum_pool(name="psum", bufs=1))
+
+        offsets = keep.tile([P, S // 16], U16, name="offsets")
+        planes = xT.rearrange("(p j) t -> j p t", j=PACK)
+        wide = [keep.tile([P, T], F32, name="wide%d" % j) for j in range(PACK)]
+        narrow = [keep.tile([P, T], BF16, name="narrow%d" % j) for j in range(PACK)]
+        picked = [keep.tile([P, V, PACK], BF16, name="picked%d" % d, align_bytes=64) for d in range(D)]
+        codes = [keep.tile([P, V], U32, name="codes%d" % d, align_bytes=64) for d in range(D)]
+        scales = [keep.tile([P, V], U8, name="scales%d" % d, align_bytes=64) for d in range(D)]
+
+        w_words, w_scales = [], []
+        for i, (words, rows) in enumerate(((w1_words, w1_scales), (w2_words, w2_scales))):
+            wt = keep.tile([P, 2 * N], U8, name="w_words%d" % i, align_bytes=64)
+            st = keep.tile([P, N], U8, name="w_scales%d" % i, align_bytes=64)
+            nc.gpsimd.dma_start(out=wt[:].bitcast(I32), in_=words[0].bitcast(I32))
+            nc.gpsimd.memset(st[:], 0)
+            for q in range(4):
+                nc.gpsimd.dma_start(out=st[32 * q : 32 * q + 4, :].bitcast(I32), in_=rows[0, 4 * q : 4 * q + 4, :].bitcast(I32))
+            w_words.append(wt)
+            w_scales.append(st)
+
+        def piece(d):
+            return offsets[:, d * (V // 16) : (d + 1) * (V // 16)]
+
+        for j in range(PACK):
+            c0 = 0
+            for width in CHUNKS[j]:
+                cols = slice(c0, c0 + width)
+                nc.sync.dma_start(out=wide[j][:, cols], in_=planes[j][:, cols])
+                if j == 0 and c0 == 0:
+                    nc.sync.dma_start(offsets[:], offs)
+                nc.vector.tensor_copy(out=narrow[j][:, cols], in_=wide[j][:, cols])
+                c0 += width
+            nc.vector.tensor_copy(out=picked[1][:, :, j], in_=wide[j][:].indirect(piece(1)))
+            nc.scalar.activation(out=picked[0][:, :, j], in_=narrow[j][:].indirect(piece(0)), func=ACT.Copy, scale=-1.0)
+            nc.scalar.activation(out=picked[2][:, :, j], in_=narrow[j][:].indirect(piece(2)), func=ACT.Copy)
+
+        for d in (1, 0, 2):
+            nc.vector.quantize_mx(out=codes[d][:].bitcast(FP8X4), scales=scales[d][:], in_=picked[d][:].rearrange("p v j -> p (v j)"))
+
+        def mx(bank, w, mb, d, start, stop):
+            nc.tensor.matmul_mx(
+                out=bank[:],
+                lhsT=w_words[w][:, 256 * mb : 256 * (mb + 1)].bitcast(FP4X4),
+                lhsT_scale=w_scales[w][:, P * mb : P * (mb + 1)],
+                rhs=codes[d][:].bitcast(FP8X4),
+                rhs_scale=scales[d][:],
+                start=start,
+                stop=stop,
+            )
+
+        def bank(tag):
+            return psum.tile([P, V], F32, name=tag, tag=tag)
+
+        def work(name):
+            return keep.tile([P, V], F32, name=name)
+
+        MB = range(N // P)
+
+        def both(name):
+            return keep.tile([P, N // P, V], F32, name=name)
+
+        th, r, ab, m, mc, xe, u0, u1, hh, f, z, rs, w, y, res = (both("t%d" % i) for i in range(15))
+        a, b, h0n, h1, h2 = {}, {}, {}, {}, {}
+        for mb in MB:
+            a[mb] = bank("a%d" % mb)
+            h1[mb] = bank("h1%d" % mb)
+            h0n[mb] = bank("h0%d" % mb)
+            b[mb] = bank("b%d" % mb)
+            mx(a[mb], 0, mb, 1, True, False)
+            if mb == 0:
+                mx(h1[mb], 1, mb, 1, True, True)
+            mx(a[mb], 0, mb, 0, False, True)
+            if mb == 0:
+                mx(h0n[mb], 1, mb, 0, True, True)
+        for mb in MB:
+            mx(b[mb], 0, mb, 0, True, False)
+            mx(b[mb], 0, mb, 2, False, True)
+            if mb == 0:
+                mx(h1[1], 1, 1, 1, True, True)
+                mx(h0n[1], 1, 1, 0, True, True)
+
+        for mb in MB:
+            nc.scalar.activation(out=th[:, mb, :], in_=a[mb][:], func=ACT.Tanh, scale=0.5)
+            nc.scalar.activation(out=r[:, mb, :], in_=a[mb][:], func=ACT.Relu)
+        for mb in MB:
+            h2[mb] = bank("a%d" % mb)
+            mx(h2[mb], 1, mb, 2, True, True)
+        for mb in MB:
+            nc.vector.scalar_tensor_tensor(out=u1[:, mb, :], in0=th[:, mb, :], scalar=1.0, in1=h1[mb][:], op0=ALU.add, op1=ALU.mult)
+            nc.vector.scalar_tensor_tensor(out=u0[:, mb, :], in0=th[:, mb, :], scalar=1.0, in1=h0n[mb][:], op0=ALU.subtract, op1=ALU.mult)
+            nc.vector.tensor_tensor(out=m[:, mb, :], in0=b[mb][:], in1=r[:, mb, :], op=ALU.subtract)
+            nc.vector.tensor_scalar(out=mc[:, mb, :], in0=m[:, mb, :], scalar1=30.0, scalar2=None, op0=ALU.min)
+            nc.scalar.activation(out=ab[:, mb, :], in_=th[:, mb, :], func=ACT.Abs)
+            nc.scalar.activation(out=xe[:, mb, :], in_=mc[:, mb, :], func=ACT.Exp)
+        for mb in MB:
+            nc.vector.scalar_tensor_tensor(out=z[:, mb, :], in0=ab[:, mb, :], scalar=1.0, in1=xe[:, mb, :], op0=ALU.add, op1=ALU.mult)
+        for mb in MB:
+            nc.vector.tensor_tensor(out=hh[:, mb, :], in0=u0[:, mb, :], in1=u1[:, mb, :], op=ALU.add)
+            nc.vector.scalar_tensor_tensor(out=f[:, mb, :], in0=hh[:, mb, :], scalar=0.5, in1=h2[mb][:], op0=ALU.mult, op1=ALU.subtract)
+
+        rows = out.rearrange("(mb p) v -> p mb v", p=P)
+        for c0 in range(0, V, V // 2):
+            cols = slice(c0, c0 + V // 2)
+            nc.scalar.activation(out=rs[:, :, cols], in_=z[:, :, cols], func=ACT.Abs_reciprocal_sqrt, scale=0.5, bias=1.0)
+            nc.scalar.activation(out=w[:, :, cols], in_=rs[:, :, cols], func=ACT.Square)
+            nc.vector.scalar_tensor_tensor(out=y[:, :, cols], in0=w[:, :, cols], scalar=1.0, in1=f[:, :, cols], op0=ALU.subtract, op1=ALU.mult)
+            nc.vector.scalar_tensor_tensor(out=res[:, :, cols], in0=hh[:, :, cols], scalar=0.5, in1=y[:, :, cols], op0=ALU.mult, op1=ALU.add)
+            nc.sync.dma_start(out=rows[:, :, cols], in_=res[:, :, cols])

@@ -19,8 +19,12 @@ ACT = mybir.ActivationFunctionType
 P = 128
 PACK = 4
 D = 3
+LIST_GROUP = 16
+W1, W2 = 0, 1
 
-CHUNKS = ([2048, 2048], [2048, 2048], [2048, 2048], [2048, 1024, 512, 512])
+PLANE_CHUNKS = ((2048, 1536, 512), (2048, 1536, 512), (2048, 1536, 512), (2048, 1024, 896, 128))
+STORE_CHUNKS = (256, 128, 128)
+LEAD_MAX = 30.0
 
 
 def tile_picked_apool_none_e_kernel(tc, xT, w1_words, w1_scales, w2_words, w2_scales, offs, out):
@@ -29,110 +33,119 @@ def tile_picked_apool_none_e_kernel(tc, xT, w1_words, w1_scales, w2_words, w2_sc
         keep = ctx.enter_context(tc.tile_pool(name="keep", bufs=1))
         psum = ctx.enter_context(tc.psum_pool(name="psum", bufs=1))
 
-        offsets = keep.tile([P, S // 16], U16, name="offsets")
-        planes = xT.rearrange("(p j) t -> j p t", j=PACK)
-        wide = [keep.tile([P, T], F32, name="wide%d" % j) for j in range(PACK)]
-        narrow = [keep.tile([P, T], BF16, name="narrow%d" % j) for j in range(PACK)]
+        offsets = keep.tile([P, S // LIST_GROUP], U16, name="offsets")
+        plane_rows = xT.rearrange("(p j) t -> j p t", j=PACK)
+        plane_f32 = [keep.tile([P, T], F32, name="plane_f32_%d" % j) for j in range(PACK)]
+        plane_bf16 = [keep.tile([P, T], BF16, name="plane_bf16_%d" % j) for j in range(PACK)]
         picked = [keep.tile([P, V, PACK], BF16, name="picked%d" % d, align_bytes=64) for d in range(D)]
         codes = [keep.tile([P, V], U32, name="codes%d" % d, align_bytes=64) for d in range(D)]
         scales = [keep.tile([P, V], U8, name="scales%d" % d, align_bytes=64) for d in range(D)]
 
-        w_words, w_scales = [], []
-        for i, (words, rows) in enumerate(((w1_words, w1_scales), (w2_words, w2_scales))):
-            wt = keep.tile([P, 2 * N], U8, name="w_words%d" % i, align_bytes=64)
-            st = keep.tile([P, N], U8, name="w_scales%d" % i, align_bytes=64)
-            nc.gpsimd.dma_start(out=wt[:].bitcast(I32), in_=words[0].bitcast(I32))
-            nc.gpsimd.memset(st[:], 0)
-            for q in range(4):
-                nc.gpsimd.dma_start(out=st[32 * q : 32 * q + 4, :].bitcast(I32), in_=rows[0, 4 * q : 4 * q + 4, :].bitcast(I32))
-            w_words.append(wt)
-            w_scales.append(st)
+        w_words = [keep.tile([P, 2 * N], U8, name="w_words%d" % w, align_bytes=64) for w in (W1, W2)]
+        w_scales = [keep.tile([P, N], U8, name="w_scales%d" % w, align_bytes=64) for w in (W1, W2)]
+        preloads = [(offsets[:], offs)]
+        for w, scale_rows in ((W1, w1_scales), (W2, w2_scales)):
+            nc.vector.memset(w_scales[w][:].bitcast(I32), 0)
+            for q in range(P // 32):
+                preloads.append((w_scales[w][32 * q : 32 * q + 4, :].bitcast(I32), scale_rows[0, 4 * q : 4 * q + 4, :].bitcast(I32)))
 
         def piece(d):
-            return offsets[:, d * (V // 16) : (d + 1) * (V // 16)]
+            return offsets[:, d * (V // LIST_GROUP) : (d + 1) * (V // LIST_GROUP)]
 
         for j in range(PACK):
             c0 = 0
-            for width in CHUNKS[j]:
+            for width in PLANE_CHUNKS[j]:
                 cols = slice(c0, c0 + width)
-                nc.sync.dma_start(out=wide[j][:, cols], in_=planes[j][:, cols])
-                if j == 0 and c0 == 0:
-                    nc.sync.dma_start(offsets[:], offs)
-                nc.vector.tensor_copy(out=narrow[j][:, cols], in_=wide[j][:, cols])
                 c0 += width
-            nc.vector.tensor_copy(out=picked[1][:, :, j], in_=wide[j][:].indirect(piece(1)))
-            nc.scalar.activation(out=picked[0][:, :, j], in_=narrow[j][:].indirect(piece(0)), func=ACT.Copy, scale=-1.0)
-            nc.scalar.activation(out=picked[2][:, :, j], in_=narrow[j][:].indirect(piece(2)), func=ACT.Copy)
+                nc.sync.dma_start(out=plane_f32[j][:, cols], in_=plane_rows[j][:, cols])
+                for dst, src in preloads[:1]:
+                    nc.sync.dma_start(dst, src)
+                preloads = preloads[1:]
+                nc.vector.tensor_copy(out=plane_bf16[j][:, cols], in_=plane_f32[j][:, cols])
+            nc.vector.tensor_copy(out=picked[1][:, :, j], in_=plane_f32[j][:].indirect(piece(1)))
+            nc.scalar.activation(out=picked[0][:, :, j], in_=plane_bf16[j][:].indirect(piece(0)), func=ACT.Copy, scale=-1.0)
+            nc.scalar.activation(out=picked[2][:, :, j], in_=plane_bf16[j][:].indirect(piece(2)), func=ACT.Copy)
+
+        for w, words in ((W1, w1_words), (W2, w2_words)):
+            nc.sync.dma_start(w_words[w][:].bitcast(I32), words[0].bitcast(I32))
 
         for d in (1, 0, 2):
             nc.vector.quantize_mx(out=codes[d][:].bitcast(FP8X4), scales=scales[d][:], in_=picked[d][:].rearrange("p v j -> p (v j)"))
 
-        def mx(bank, w, mb, d, start, stop):
-            nc.tensor.matmul_mx(
-                out=bank[:],
-                lhsT=w_words[w][:, 256 * mb : 256 * (mb + 1)].bitcast(FP4X4),
-                lhsT_scale=w_scales[w][:, P * mb : P * (mb + 1)],
-                rhs=codes[d][:].bitcast(FP8X4),
-                rhs_scale=scales[d][:],
-                start=start,
-                stop=stop,
-            )
+        def product(tag, w, rb, pieces):
+            acc = psum.tile([P, V], F32, name=tag, tag=tag)
+            for i, d in enumerate(pieces):
+                nc.tensor.matmul_mx(
+                    out=acc[:],
+                    lhsT=w_words[w][:, 2 * P * rb : 2 * P * (rb + 1)].bitcast(FP4X4),
+                    lhsT_scale=w_scales[w][:, P * rb : P * (rb + 1)],
+                    rhs=codes[d][:].bitcast(FP8X4),
+                    rhs_scale=scales[d][:],
+                    start=(i == 0),
+                    stop=(i == len(pieces) - 1),
+                )
+            return acc
 
-        def bank(tag):
-            return psum.tile([P, V], F32, name=tag, tag=tag)
+        blocks = range(N // P)
 
-        def work(name):
-            return keep.tile([P, V], F32, name=name)
-
-        MB = range(N // P)
-
-        def both(name):
+        def values(name):
             return keep.tile([P, N // P, V], F32, name=name)
 
-        th, r, ab, m, mc, xe, u0, u1, hh, f, z, rs, w, y, res = (both("t%d" % i) for i in range(15))
-        a, b, h0n, h1, h2 = {}, {}, {}, {}, {}
-        for mb in MB:
-            a[mb] = bank("a%d" % mb)
-            h1[mb] = bank("h1%d" % mb)
-            h0n[mb] = bank("h0%d" % mb)
-            b[mb] = bank("b%d" % mb)
-            mx(a[mb], 0, mb, 1, True, False)
-            if mb == 0:
-                mx(h1[mb], 1, mb, 1, True, True)
-            mx(a[mb], 0, mb, 0, False, True)
-            if mb == 0:
-                mx(h0n[mb], 1, mb, 0, True, True)
-        for mb in MB:
-            mx(b[mb], 0, mb, 0, True, False)
-            mx(b[mb], 0, mb, 2, False, True)
-            if mb == 0:
-                mx(h1[1], 1, 1, 1, True, True)
-                mx(h0n[1], 1, 1, 0, True, True)
+        t, relu_a, abs_t = values("t"), values("relu_a"), values("abs_t")
+        lead, lead_cut, exp_lead, z = values("lead"), values("lead_cut"), values("exp_lead"), values("z")
+        part0, part1, pair = values("part0"), values("part1"), values("pair")
+        z_h2, numerator, root, weight, result = values("z_h2"), values("numerator"), values("root"), values("weight"), values("result")
 
-        for mb in MB:
-            nc.scalar.activation(out=th[:, mb, :], in_=a[mb][:], func=ACT.Tanh, scale=0.5)
-            nc.scalar.activation(out=r[:, mb, :], in_=a[mb][:], func=ACT.Relu)
-        for mb in MB:
-            h2[mb] = bank("a%d" % mb)
-            mx(h2[mb], 1, mb, 2, True, True)
-        for mb in MB:
-            nc.vector.scalar_tensor_tensor(out=u1[:, mb, :], in0=th[:, mb, :], scalar=1.0, in1=h1[mb][:], op0=ALU.add, op1=ALU.mult)
-            nc.vector.scalar_tensor_tensor(out=u0[:, mb, :], in0=th[:, mb, :], scalar=1.0, in1=h0n[mb][:], op0=ALU.subtract, op1=ALU.mult)
-            nc.vector.tensor_tensor(out=m[:, mb, :], in0=b[mb][:], in1=r[:, mb, :], op=ALU.subtract)
-            nc.vector.tensor_scalar(out=mc[:, mb, :], in0=m[:, mb, :], scalar1=30.0, scalar2=None, op0=ALU.min)
-            nc.scalar.activation(out=ab[:, mb, :], in_=th[:, mb, :], func=ACT.Abs)
-            nc.scalar.activation(out=xe[:, mb, :], in_=mc[:, mb, :], func=ACT.Exp)
-        for mb in MB:
-            nc.vector.scalar_tensor_tensor(out=z[:, mb, :], in0=ab[:, mb, :], scalar=1.0, in1=xe[:, mb, :], op0=ALU.add, op1=ALU.mult)
-        for mb in MB:
-            nc.vector.tensor_tensor(out=hh[:, mb, :], in0=u0[:, mb, :], in1=u1[:, mb, :], op=ALU.add)
-            nc.vector.scalar_tensor_tensor(out=f[:, mb, :], in0=hh[:, mb, :], scalar=0.5, in1=h2[mb][:], op0=ALU.mult, op1=ALU.subtract)
+        a0 = product("a0", W1, 0, (1, 0))
+        h1_0 = product("h1", W2, 0, (1,))
+        minus_h0_0 = product("minus_h0", W2, 0, (0,))
+        a1 = product("a1", W1, 1, (0, 1))
+        b = [product("b%d" % rb, W1, rb, (0, 2)) for rb in blocks]
 
-        rows = out.rearrange("(mb p) v -> p mb v", p=P)
-        for c0 in range(0, V, V // 2):
-            cols = slice(c0, c0 + V // 2)
-            nc.scalar.activation(out=rs[:, :, cols], in_=z[:, :, cols], func=ACT.Abs_reciprocal_sqrt, scale=0.5, bias=1.0)
-            nc.scalar.activation(out=w[:, :, cols], in_=rs[:, :, cols], func=ACT.Square)
-            nc.vector.scalar_tensor_tensor(out=y[:, :, cols], in0=w[:, :, cols], scalar=1.0, in1=f[:, :, cols], op0=ALU.subtract, op1=ALU.mult)
-            nc.vector.scalar_tensor_tensor(out=res[:, :, cols], in0=hh[:, :, cols], scalar=0.5, in1=y[:, :, cols], op0=ALU.mult, op1=ALU.add)
-            nc.sync.dma_start(out=rows[:, :, cols], in_=res[:, :, cols])
+        nc.scalar.activation(out=t[:, 0, :], in_=a0[:], func=ACT.Tanh, scale=0.5)
+        nc.scalar.activation(out=relu_a[:, 0, :], in_=a0[:], func=ACT.Relu)
+        nc.scalar.activation(out=abs_t[:, 0, :], in_=t[:, 0, :], func=ACT.Abs)
+        nc.scalar.activation(out=relu_a[:, 1, :], in_=a1[:], func=ACT.Relu)
+        nc.scalar.activation(out=t[:, 1, :], in_=a1[:], func=ACT.Tanh, scale=0.5)
+
+        nc.vector.scalar_tensor_tensor(out=part1[:, 0, :], in0=t[:, 0, :], scalar=1.0, in1=h1_0[:], op0=ALU.add, op1=ALU.mult)
+        nc.vector.scalar_tensor_tensor(out=part0[:, 0, :], in0=t[:, 0, :], scalar=1.0, in1=minus_h0_0[:], op0=ALU.subtract, op1=ALU.mult)
+
+        h1_less_h0_1 = product("h1", W2, 1, (0, 1))
+        minus_h0_1 = product("minus_h0", W2, 1, (0,))
+        h2 = [product("h2_%d" % rb, W2, rb, (2,)) for rb in blocks]
+
+        nc.gpsimd.tensor_tensor(out=pair[:, 0, :], in0=part0[:, 0, :], in1=part1[:, 0, :], op=ALU.add)
+        for rb in blocks:
+            nc.vector.tensor_tensor(out=lead[:, rb, :], in0=b[rb][:], in1=relu_a[:, rb, :], op=ALU.subtract)
+        for rb in blocks:
+            nc.vector.tensor_scalar(out=lead_cut[:, rb, :], in0=lead[:, rb, :], scalar1=LEAD_MAX, scalar2=None, op0=ALU.min)
+        nc.scalar.activation(out=abs_t[:, 1, :], in_=t[:, 1, :], func=ACT.Abs)
+        for rb in blocks:
+            nc.scalar.activation(out=exp_lead[:, rb, :], in_=lead_cut[:, rb, :], func=ACT.Exp)
+
+        def make_z(rb):
+            nc.vector.scalar_tensor_tensor(out=z[:, rb, :], in0=abs_t[:, rb, :], scalar=1.0, in1=exp_lead[:, rb, :], op0=ALU.add, op1=ALU.mult)
+
+        nc.vector.scalar_tensor_tensor(out=part1[:, 1, :], in0=t[:, 1, :], scalar=1.0, in1=h1_less_h0_1[:], op0=ALU.add, op1=ALU.mult)
+        make_z(0)
+        nc.vector.scalar_tensor_tensor(out=pair[:, 1, :], in0=minus_h0_1[:], scalar=-2.0, in1=part1[:, 1, :], op0=ALU.mult, op1=ALU.add)
+        make_z(1)
+        for rb in blocks:
+            nc.vector.tensor_tensor(out=z_h2[:, rb, :], in0=h2[rb][:], in1=z[:, rb, :], op=ALU.mult)
+
+        halves = (slice(0, V // 2), slice(V // 2, V))
+        for cols in halves:
+            nc.scalar.activation(out=root[:, :, cols], in_=z[:, :, cols], func=ACT.Abs_reciprocal_sqrt, scale=0.5, bias=1.0)
+        for cols in halves:
+            nc.scalar.activation(out=weight[:, :, cols], in_=root[:, :, cols], func=ACT.Square)
+        for rb in blocks:
+            nc.vector.tensor_tensor(out=numerator[:, rb, :], in0=z_h2[:, rb, :], in1=pair[:, rb, :], op=ALU.add)
+
+        out_rows = out.rearrange("(rb p) v -> p rb v", p=P)
+        c0 = 0
+        for width in STORE_CHUNKS:
+            cols = slice(c0, c0 + width)
+            c0 += width
+            nc.vector.scalar_tensor_tensor(out=result[:, :, cols], in0=numerator[:, :, cols], scalar=0.5, in1=weight[:, :, cols], op0=ALU.mult, op1=ALU.mult)
+            nc.sync.dma_start(out=out_rows[:, :, cols], in_=result[:, :, cols])

from contextlib import ExitStack

import concourse.mybir as mybir

K, T, S, V, N = 512, 4096, 1536, 512, 256
FLOPS = 2 * K * S * 2 * N

F32 = mybir.dt.float32
BF16 = mybir.dt.bfloat16
I32 = mybir.dt.int32
U32 = mybir.dt.uint32
U16 = mybir.dt.uint16
U8 = mybir.dt.uint8
FP8X4 = mybir.dt.float8_e4m3fn_x4
FP4X4 = mybir.dt.float4_e2m1fn_x4
ALU = mybir.AluOpType
ACT = mybir.ActivationFunctionType

P = 128
PACK = 4
D = 3
LIST_GROUP = 16
W1, W2 = 0, 1

PLANE_CHUNKS = ((2048, 1536, 512), (2048, 1536, 512), (2048, 1536, 512), (2048, 1024, 896, 128))
STORE_CHUNKS = (256, 128, 128)
LEAD_MAX = 30.0


def tile_picked_apool_none_e_kernel(tc, xT, w1_words, w1_scales, w2_words, w2_scales, offs, out):
    nc = tc.nc
    with ExitStack() as ctx:
        keep = ctx.enter_context(tc.tile_pool(name="keep", bufs=1))
        psum = ctx.enter_context(tc.psum_pool(name="psum", bufs=1))

        offsets = keep.tile([P, S // LIST_GROUP], U16, name="offsets")
        plane_rows = xT.rearrange("(p j) t -> j p t", j=PACK)
        plane_f32 = [keep.tile([P, T], F32, name="plane_f32_%d" % j) for j in range(PACK)]
        plane_bf16 = [keep.tile([P, T], BF16, name="plane_bf16_%d" % j) for j in range(PACK)]
        picked = [keep.tile([P, V, PACK], BF16, name="picked%d" % d, align_bytes=64) for d in range(D)]
        codes = [keep.tile([P, V], U32, name="codes%d" % d, align_bytes=64) for d in range(D)]
        scales = [keep.tile([P, V], U8, name="scales%d" % d, align_bytes=64) for d in range(D)]

        w_words = [keep.tile([P, 2 * N], U8, name="w_words%d" % w, align_bytes=64) for w in (W1, W2)]
        w_scales = [keep.tile([P, N], U8, name="w_scales%d" % w, align_bytes=64) for w in (W1, W2)]
        preloads = [(offsets[:], offs)]
        for w, scale_rows in ((W1, w1_scales), (W2, w2_scales)):
            nc.vector.memset(w_scales[w][:].bitcast(I32), 0)
            for q in range(P // 32):
                preloads.append((w_scales[w][32 * q : 32 * q + 4, :].bitcast(I32), scale_rows[0, 4 * q : 4 * q + 4, :].bitcast(I32)))

        def piece(d):
            return offsets[:, d * (V // LIST_GROUP) : (d + 1) * (V // LIST_GROUP)]

        for j in range(PACK):
            c0 = 0
            for width in PLANE_CHUNKS[j]:
                cols = slice(c0, c0 + width)
                c0 += width
                nc.sync.dma_start(out=plane_f32[j][:, cols], in_=plane_rows[j][:, cols])
                for dst, src in preloads[:1]:
                    nc.sync.dma_start(dst, src)
                preloads = preloads[1:]
                nc.vector.tensor_copy(out=plane_bf16[j][:, cols], in_=plane_f32[j][:, cols])
            nc.vector.tensor_copy(out=picked[1][:, :, j], in_=plane_f32[j][:].indirect(piece(1)))
            nc.scalar.activation(out=picked[0][:, :, j], in_=plane_bf16[j][:].indirect(piece(0)), func=ACT.Copy, scale=-1.0)
            nc.scalar.activation(out=picked[2][:, :, j], in_=plane_bf16[j][:].indirect(piece(2)), func=ACT.Copy)

        for w, words in ((W1, w1_words), (W2, w2_words)):
            nc.sync.dma_start(w_words[w][:].bitcast(I32), words[0].bitcast(I32))

        for d in (1, 0, 2):
            nc.vector.quantize_mx(out=codes[d][:].bitcast(FP8X4), scales=scales[d][:], in_=picked[d][:].rearrange("p v j -> p (v j)"))

        def product(tag, w, rb, pieces):
            acc = psum.tile([P, V], F32, name=tag, tag=tag)
            for i, d in enumerate(pieces):
                nc.tensor.matmul_mx(
                    out=acc[:],
                    lhsT=w_words[w][:, 2 * P * rb : 2 * P * (rb + 1)].bitcast(FP4X4),
                    lhsT_scale=w_scales[w][:, P * rb : P * (rb + 1)],
                    rhs=codes[d][:].bitcast(FP8X4),
                    rhs_scale=scales[d][:],
                    start=(i == 0),
                    stop=(i == len(pieces) - 1),
                )
            return acc

        blocks = range(N // P)

        def values(name):
            return keep.tile([P, N // P, V], F32, name=name)

        t, relu_a, abs_t = values("t"), values("relu_a"), values("abs_t")
        lead, lead_cut, exp_lead, z = values("lead"), values("lead_cut"), values("exp_lead"), values("z")
        part0, part1, pair = values("part0"), values("part1"), values("pair")
        z_h2, numerator, root, weight, result = values("z_h2"), values("numerator"), values("root"), values("weight"), values("result")

        a0 = product("a0", W1, 0, (1, 0))
        h1_0 = product("h1", W2, 0, (1,))
        minus_h0_0 = product("minus_h0", W2, 0, (0,))
        a1 = product("a1", W1, 1, (0, 1))
        b = [product("b%d" % rb, W1, rb, (0, 2)) for rb in blocks]

        nc.scalar.activation(out=t[:, 0, :], in_=a0[:], func=ACT.Tanh, scale=0.5)
        nc.scalar.activation(out=relu_a[:, 0, :], in_=a0[:], func=ACT.Relu)
        nc.scalar.activation(out=abs_t[:, 0, :], in_=t[:, 0, :], func=ACT.Abs)
        nc.scalar.activation(out=relu_a[:, 1, :], in_=a1[:], func=ACT.Relu)
        nc.scalar.activation(out=t[:, 1, :], in_=a1[:], func=ACT.Tanh, scale=0.5)

        nc.vector.scalar_tensor_tensor(out=part1[:, 0, :], in0=t[:, 0, :], scalar=1.0, in1=h1_0[:], op0=ALU.add, op1=ALU.mult)
        nc.vector.scalar_tensor_tensor(out=part0[:, 0, :], in0=t[:, 0, :], scalar=1.0, in1=minus_h0_0[:], op0=ALU.subtract, op1=ALU.mult)

        h1_less_h0_1 = product("h1", W2, 1, (0, 1))
        minus_h0_1 = product("minus_h0", W2, 1, (0,))
        h2 = [product("h2_%d" % rb, W2, rb, (2,)) for rb in blocks]

        nc.gpsimd.tensor_tensor(out=pair[:, 0, :], in0=part0[:, 0, :], in1=part1[:, 0, :], op=ALU.add)
        for rb in blocks:
            nc.vector.tensor_tensor(out=lead[:, rb, :], in0=b[rb][:], in1=relu_a[:, rb, :], op=ALU.subtract)
        for rb in blocks:
            nc.vector.tensor_scalar(out=lead_cut[:, rb, :], in0=lead[:, rb, :], scalar1=LEAD_MAX, scalar2=None, op0=ALU.min)
        nc.scalar.activation(out=abs_t[:, 1, :], in_=t[:, 1, :], func=ACT.Abs)
        for rb in blocks:
            nc.scalar.activation(out=exp_lead[:, rb, :], in_=lead_cut[:, rb, :], func=ACT.Exp)

        def make_z(rb):
            nc.vector.scalar_tensor_tensor(out=z[:, rb, :], in0=abs_t[:, rb, :], scalar=1.0, in1=exp_lead[:, rb, :], op0=ALU.add, op1=ALU.mult)

        nc.vector.scalar_tensor_tensor(out=part1[:, 1, :], in0=t[:, 1, :], scalar=1.0, in1=h1_less_h0_1[:], op0=ALU.add, op1=ALU.mult)
        make_z(0)
        nc.vector.scalar_tensor_tensor(out=pair[:, 1, :], in0=minus_h0_1[:], scalar=-2.0, in1=part1[:, 1, :], op0=ALU.mult, op1=ALU.add)
        make_z(1)
        for rb in blocks:
            nc.vector.tensor_tensor(out=z_h2[:, rb, :], in0=h2[rb][:], in1=z[:, rb, :], op=ALU.mult)

        halves = (slice(0, V // 2), slice(V // 2, V))
        for cols in halves:
            nc.scalar.activation(out=root[:, :, cols], in_=z[:, :, cols], func=ACT.Abs_reciprocal_sqrt, scale=0.5, bias=1.0)
        for cols in halves:
            nc.scalar.activation(out=weight[:, :, cols], in_=root[:, :, cols], func=ACT.Square)
        for rb in blocks:
            nc.vector.tensor_tensor(out=numerator[:, rb, :], in0=z_h2[:, rb, :], in1=pair[:, rb, :], op=ALU.add)

        out_rows = out.rearrange("(rb p) v -> p rb v", p=P)
        c0 = 0
        for width in STORE_CHUNKS:
            cols = slice(c0, c0 + width)
            c0 += width
            nc.vector.scalar_tensor_tensor(out=result[:, :, cols], in0=numerator[:, :, cols], scalar=0.5, in1=weight[:, :, cols], op0=ALU.mult, op1=ALU.mult)
            nc.sync.dma_start(out=out_rows[:, :, cols], in_=result[:, :, cols])
